import numpy as np, ml_dtypes
CORES = [51,54,179,182]
N = 4
import mx_ref
BF = ml_dtypes.bfloat16
def entries(a):
    return np.ascontiguousarray(a.T).reshape(-1)
def table(e):
    return np.ascontiguousarray(np.reshape(e, (-1, 16)).T).astype(np.int32)
def gpick(z, e):
    return np.concatenate([z[16 * g:16 * g + 16][:, e[g]] for g in range(8)])
def tile(rs):
    return np.stack(rs, axis=2).reshape(128, -1).astype(BF)
def cut(t, i, w=512):
    return t[:, w * i:w * i + w]
def f(rng, *shape):
    return mx_ref.flush((rng.standard_normal(shape, dtype=np.float32) * np.exp2(rng.integers(-2, 3, shape[:-1] + (1,)))).astype(BF))
def wide(rng, *shape, cols=0):
    v = rng.standard_normal(shape, dtype=np.float32) * np.exp2(rng.integers(-12, 13, shape)).astype(np.float32)
    if cols: v *= np.repeat(np.exp2(rng.integers(-cols, cols + 1, shape[:-2] + (1, shape[-1] // 4))) * (rng.random(shape[:-2] + (1, shape[-1] // 4)) > 0.0625), 4, axis=-1).astype(np.float32)
    return mx_ref.flush(v.astype(BF))
TQ, O = 256, 1
def lay(k, q):
    return {"kp": np.repeat(k, 16, axis=1).astype(np.int32), "qp": np.stack([table(e) for e in q])}
def setup_inputs(rng):
    d = {"qx": f(rng, N, 128, 4 * TQ), "ky": f(rng, N, 128, 2048), "rt": np.repeat(f(rng, 1, 128, 1024), N, axis=0), "vv": f(rng, N, 128, 512 * O)}
    a = rng.integers(0, 3585)
    k = a + rng.integers(0, 512, (N, 8, 4))
    q = np.where(rng.random((N, TQ)) < 0.25, rng.integers(0, 4096, (N, TQ)), a + rng.integers(0, 512, (N, TQ)))
    return {**d, **lay(k, q)}
def setup_inputs_far(rng):
    d = setup_inputs(rng)
    k = rng.integers(1500, 2501, (N, 32)); q = np.zeros((N, TQ), int); a = int(rng.integers(0, 2))
    for r in range(N):
        k[r, rng.permutation(32)[:2]] = [1500, 2500]
        lo, hi = (2628, 4095) if (r + a) % 2 else (0, 1371)
        q[r] = rng.integers(lo, hi + 1, TQ)
        q[r, rng.permutation(TQ)[:2]] = [lo, hi]
    return {**d, **lay(k.reshape(N, 8, 4), q)}
def setup_inputs_same(rng):
    d = setup_inputs(rng); a = int(rng.integers(0, 4096))
    return {**d, **lay(np.full((N, 8, 4), a), np.full((N, TQ), a))}
def setup_inputs_descending(rng):
    d = setup_inputs(rng); a = rng.integers(0, 3585)
    q = np.stack([a + np.sort(rng.permutation(512)[:TQ])[::-1] for r in range(N)])
    k = np.stack([a + 16 * rng.permutation(32) + rng.integers(0, 16, 32) for r in range(N)])
    return {**d, **lay(k.reshape(N, 8, 4), q)}
def setup_inputs_near(rng):
    d = setup_inputs(rng); a = rng.integers(2049, 3968)
    q = np.stack([a + rng.permutation(TQ) % 128 for r in range(N)])
    k = np.stack([a + rng.permutation(np.concatenate([[0, 128], 1 + rng.permutation(127)[:30]])) for r in range(N)])
    return {**d, **lay(k.reshape(N, 8, 4), q)}
def setup_inputs_spread(rng):
    d = setup_inputs(rng); d["qx"] = wide(rng, N, 128, 4 * TQ, cols=4); return d
def check_inputs(d):
    b = []
    for r in range(N):
        k, q = d["kp"][r], entries(d["qp"][r])
        if d["rt"][r].tobytes() != d["rt"][0].tobytes(): b.append("rt")
        if k.min() < 0 or k.max() > 4095 or (k != np.repeat(k[::16], 16, axis=0)).any(): b.append("kp")
        if q.min() < 0 or q.max() > 4095: b.append("qp")
    return b
def reference(qx, ky, rt, vv, kp, qp):
    y = np.zeros((N, 128, O * TQ), np.float32)
    X = [mx_ref.quantize(qx[r]) for r in range(N)]
    for s in range(N):
        K = [mx_ref.quantize(np.ascontiguousarray(cut(ky[s], b))) for b in range(4)]
        V = [mx_ref.quantize(np.ascontiguousarray(cut(vv[s], o))) for o in range(O)]
        R = mx_ref.quantize(rt[s])
        P = [mx_ref.matmul(K[b], R) for b in range(4)]
        for r in range(N):
            A = []
            for b in range(4):
                c = np.clip(entries(qp[r])[None, :] - kp[s][::16, b][:, None], -128, 127) + 128
                A.append(np.maximum(mx_ref.matmul(K[b], X[r]) + gpick(P[b], c), np.float32(0)) * np.float32(0.03125))
            A = mx_ref.quantize(tile(A))
            for o in range(O): y[r][:, TQ * o:TQ * o + TQ] += mx_ref.matmul(V[o], A)
    return {"y": y}

@@ -1,0 +1,281 @@
+from concourse.bass import DstId, RemoteDMATransfer
+from concourse.mybir import dt, AluOpType, ActivationFunctionType
+
+CODES = "float8_e4m3fn_x4"
+SCRATCH = {
+    "ky_b": ("sbuf", [128, 2048], "bfloat16"),
+    "qx_b": ("sbuf", [128, 1024], "bfloat16"),
+    "rt_b": ("sbuf", [128, 1024], "bfloat16"),
+    "vv_b": ("sbuf", [128, 512], "bfloat16"),
+    "pz": ("sbuf", [128, 20], "int32"),
+    "pu": ("sbuf", [128, 20], "uint16"),
+    "pt": ("sbuf", [128, 20], "uint16"),
+    "ph": ("sbuf", [128, 20], "uint16"),
+    "pp": ("sbuf", [128, 20], "uint16"),
+    "kf": ("sbuf", [128, 4], "float32"),
+    "of0": ("sbuf", [128, 64], "uint16"),
+    "of1": ("sbuf", [128, 64], "uint16"),
+    "kq0": ("sbuf", [128, 512], CODES), "ks0": ("sbuf", [128, 512], "uint8"),
+    "kq1": ("sbuf", [128, 512], CODES), "ks1": ("sbuf", [128, 512], "uint8"),
+    "xq0": ("sbuf", [128, 256], CODES), "xs0": ("sbuf", [128, 256], "uint8"),
+    "xq1": ("sbuf", [128, 256], CODES), "xs1": ("sbuf", [128, 256], "uint8"),
+    "rq": ("sbuf", [128, 256], CODES), "rs": ("sbuf", [128, 256], "uint8"),
+    "pw": ("sbuf", [128, 1024], "float32"),
+    "yo": ("sbuf", [128, 256], "float32"),
+}
+for _i in range(4):
+    SCRATCH["vq%d" % _i] = ("sbuf", [128, 128], CODES)
+    SCRATCH["vs%d" % _i] = ("sbuf", [128, 128], "uint8")
+for _p in range(2):
+    SCRATCH["u%d" % _p] = ("sbuf", [128, 1024], "float32")
+    SCRATCH["a%d" % _p] = ("sbuf", [128, 1024], "bfloat16")
+    SCRATCH["aq%d" % _p] = ("sbuf", [128, 256], CODES)
+    SCRATCH["as%d" % _p] = ("sbuf", [128, 256], "uint8")
+for _p in "pth":
+    SCRATCH["bq_" + _p] = ("sbuf", [128, 256], CODES)
+    SCRATCH["bs_" + _p] = ("sbuf", [128, 256], "uint8")
+for _i in range(8):
+    SCRATCH["ps%d" % _i] = ("psum", [128, 512], "float32")
+
+SEMAPHORES = (["l_ky0", "l_ky1", "l_qx", "l_rt", "l_vv", "l_pos", "q_ky0", "q_ky1", "q_qx", "q_rt", "q_vv", "pu", "kf",
+               "n_pt", "n_ph", "n_pp", "n_k0", "n_k1", "n_r", "n_x", "n_v1", "n_v2", "n_v3", "n_ap", "n_at", "n_ah", "sent",
+               "ydone", "ycopy", "ystore", "q0", "q1"]
+              + ["p%d" % b for b in range(4)] + ["c%d" % b for b in range(4)]
+              + ["%s%d_%d" % (k, p, b) for k in "osgdr" for p in range(2) for b in range(4)])
+
+LOADS = ["ky0", "rt", "ky1", "qx", "vv"]
+QUANTS = ["ky0", "rt", "ky1", "qx"]
+SENDS = ["k0", "r", "k1", "x", "v"]
+TENSOR = ["p0 p1 s00 s01 p2 p3 s02 s03 s10 s11 s12 s13", "p0 p1 s%0 s%1 p2 p3 s%2 s%3"]
+SCALAR = ["c0 g00 g01 c2 g02 g03 g10 g11 g12 g13 r10 r11 r12", "c0 g%0 c2 g%2 r%0 r%1 r%2"]
+VECTOR = ["kf o00 o01 o02 o03 c1 d00 r00 d01 r01 c3 qvv o10 o11 o12 o13 d02 r02 d03 r03 q0 d10 d11 d12 d13 r13 q1",
+          "kf o%0 o%1 o%2 o%3 c1 g%1 d%0 d%1 c3 g%3 d%2 d%3 r%3 q%"]
+YORDER = ["own", "p", "t", "h"]
+
+
+def rank_program(g, core, T, topo):
+    here = topo.cores_of(core)
+    ranks = [c for c in T.cores if c in here]
+    if not ranks:
+        return
+
+    def team(r):
+        return [r] + [c for c in topo.cores_of(r) if topo.die(c) == topo.die(r) and c != r][:2]
+
+    own = [c for c in ranks if topo.die(c) == topo.die(core)][0]
+    if core not in team(own):
+        return
+    role = team(own).index(core)
+    is_rank = role == 0
+    partner = [c for c in ranks if c != own][0]
+    far = [c for c in T.cores if c not in here]
+    twin = [c for c in far if topo.die(c) == topo.die(own)][0]
+    diag = [c for c in far if c != twin][0]
+    off = topo.engines(own, twin)
+    every = topo.engines(own, partner)
+    on = [e for e in every if e not in off]
+    half = len(off) // 2
+
+    direct = role == 1
+    count = {"l_pos": 9 * 16, "ystore": 16, "n_pt": len(off if direct else every), "n_ph": half, "n_pp": len(every) if is_rank else half,
+             "n_k0": 2 * len(off if direct else every), "n_k1": 2 * len(off if direct else every), "n_r": 2 * len(on if direct else every),
+             "n_x": 2 * (len(off) if is_rank else half), "n_v1": 2 * len(on), "n_v2": 2 * half, "n_v3": 2 * half}
+    for n in ("n_ap", "n_at", "n_ah"):
+        count[n] = 2 * len(every)
+    for n in LOADS:
+        count["l_" + n] = 16
+    seen = set()
+
+    def need(queue, tag, *events):
+        for e in events:
+            if (tag, e) not in seen:
+                seen.add((tag, e))
+                queue.wait_ge(T.sem[e], count.get(e, 1))
+
+    V, S, E = g.vector, g.scalar, g.tensor
+    sent = [0]
+
+    def xfer(dst, engines, sem, out, src):
+        rid, pid = topo.addr(dst, core)
+        sent[0] += len(engines)
+        return RemoteDMATransfer(dst_ids=[DstId(rid=rid, pnc=pid)], dma_engine_mask=sum(1 << e for e in engines), remote_sem=T.sem[sem], srcs=[src], dsts=[out])
+
+    def fused(*transfers):
+        g.remote_dma_fused(list(transfers), local_sem=T.sem.sent)
+
+    def view(n, name, lo, hi):
+        return T[name % n][:, lo:hi].bitcast(dt.uint8) if n == "q" else T[name % n][:, lo:hi]
+
+    def put(n, dst, engines, sem, out, src, lo=0, hi=256):
+        return xfer(dst, engines, sem, view(n, out, lo, hi), view(n, src, lo, hi))
+
+    def positions(dst, engines, sem, out, src):
+        return xfer(dst, engines, sem, T[out][:, 0:20], T[src][:, 0:20])
+
+    def tile_out(p, dst, key):
+        need(g, "g", "q%d" % p)
+        for n in "qs":
+            fused(put(n, dst, every, "n_a" + key, "b%s_" + key, "a%s" + str(p)))
+
+    def send(what):
+        if what in ("k0", "k1"):
+            need(g, "g", "q_ky" + what[1])
+            lo = 256 * int(what[1])
+            for n in "qs":
+                fused(put(n, team(twin)[1], off, "n_" + what, "k%s1", "k%s0", lo, lo + 256))
+        if what == "r":
+            need(g, "g", "q_rt")
+            for n in "qs":
+                fused(put(n, team(own)[1], on, "n_r", "r%s", "r%s"))
+        if what == "x":
+            need(g, "g", "q_qx")
+            for n in "qs":
+                fused(put(n, team(own)[1], on[:half], "n_x", "x%s0", "x%s0"), put(n, team(partner)[2], on[half:], "n_x", "x%s1", "x%s0"),
+                      put(n, partner, off, "n_x", "x%s1", "x%s0"))
+        if what == "v":
+            need(g, "g", "q_vv")
+            for n in "qs":
+                fused(put(n, twin, off[:half], "n_v2", "v%s2", "v%s0", 0, 128), put(n, diag, off[half:], "n_v3", "v%s3", "v%s0", 0, 128),
+                      put(n, partner, on, "n_v1", "v%s1", "v%s0", 0, 128))
+
+    if is_rank:
+        g.sync.dma_start(T.pz[:, 0:4], T.kp[:]).then_inc(T.sem["l_pos"], 16)
+        for i in range(8):
+            (S if i % 2 else g.sync).dma_start(T.pz[16 * i:16 * i + 16, 4:20], T.qp[:]).then_inc(T.sem["l_pos"], 16)
+        for n in LOADS:
+            out, src = {"ky0": (T.ky_b[:, 0:1024], T.ky[:, 0:1024]), "ky1": (T.ky_b[:, 1024:2048], T.ky[:, 1024:2048]), "rt": (T.rt_b[:], T.rt[:]),
+                        "qx": (T.qx_b[:], T.qx[:]), "vv": (T.vv_b[:], T.vv[:])}[n]
+            S.dma_start(out, src).then_inc(T.sem["l_" + n], 16)
+
+    def quant(name):
+        need(V, "V", "l_" + name)
+        q, s, b, lo, n = {"ky0": ("kq0", "ks0", "ky_b", 0, 256), "ky1": ("kq0", "ks0", "ky_b", 256, 256), "qx": ("xq0", "xs0", "qx_b", 0, 256),
+                          "rt": ("rq", "rs", "rt_b", 0, 256), "vv": ("vq0", "vs0", "vv_b", 0, 128)}[name]
+        V.quantize_mx(T[q][:, lo:lo + n], T[s][:, lo:lo + n], T[b][:, 4 * lo:4 * lo + 4 * n]).then_inc(T.sem["q_" + name], 1)
+
+    KQ, KS = (T.kq0, T.ks0) if is_rank else (T.kq1, T.ks1)
+    key_pos = (T.pu, "pu") if is_rank else (T.pt, "n_pt")
+    query_pos = ((T.pu, "pu") if is_rank else (T.ph, "n_ph"), (T.pp, "n_pp"))
+    query_ready = ("q_qx" if is_rank else "n_x", "n_x")
+    rt_ready = "q_rt" if is_rank else "n_r"
+    held, turn, bank = {}, {"p": 0, "s": 0}, {}
+
+    def keypos():
+        need(V, "V", key_pos[1])
+        V.tensor_scalar(T.kf[:], key_pos[0][:, 0:4], 128.0, None, AluOpType.subtract).then_inc(T.sem.kf, 1)
+
+    def offsets(p, b):
+        need(V, "V", query_pos[p][1], "kf")
+        V.tensor_scalar(T["of%d" % p][:, 16 * b:16 * b + 16], query_pos[p][0][:, 4:20], T.kf[:, b:b + 1], 255.0,
+                        AluOpType.subtract, AluOpType.min).then_inc(T.sem["o%d_%d" % (p, b)], 1)
+
+    def product(kind, banks, name, free, b, moving, ready):
+        k = banks[turn[kind] % len(banks)]
+        turn[kind] += 1
+        if k in held:
+            need(E, "E", held[k])
+        held[k] = free
+        bank[name] = T["ps%d" % k]
+        need(E, "E", ready, ("q_ky%d" if is_rank else "n_k%d") % (b // 2))
+        E.matmul_mx(bank[name][:, 0:256], KQ[:, 128 * b:128 * b + 128], KS[:, 128 * b:128 * b + 128],
+                    T[moving % "q"][:, 0:256], T[moving % "s"][:, 0:256], True, True).then_inc(T.sem[name], 1)
+
+    def copy_p(q, b):
+        need(V if q == "V" else S, q, "p%d" % b)
+        out, src = T.pw[:, 256 * b:256 * b + 256], bank["p%d" % b][:, 0:256]
+        i = V.tensor_copy(out, src) if q == "V" else S.activation(out, src, ActivationFunctionType.Copy)
+        i.then_inc(T.sem["c%d" % b], 1)
+
+    def pick(q, p, b):
+        out = T["u%d" % p][:, 256 * b:256 * b + 256]
+        src = T.pw[:, 256 * b:256 * b + 256].indirect(T["of%d" % p][:, 16 * b:16 * b + 16])
+        need(V if q == "V" else S, q, "c%d" % b, "o%d_%d" % (p, b))
+        i = V.tensor_copy(out, src) if q == "V" else S.activation(out, src, ActivationFunctionType.Copy)
+        i.then_inc(T.sem["g%d_%d" % (p, b)], 1)
+
+    def add(p, b):
+        need(V, "V", "s%d_%d" % (p, b), "g%d_%d" % (p, b))
+        V.tensor_tensor(T["a%d" % p][:, b:1024:4], bank["s%d_%d" % (p, b)][:, 0:256], T["u%d" % p][:, 256 * b:256 * b + 256],
+                        AluOpType.add).then_inc(T.sem["d%d_%d" % (p, b)], 1)
+
+    def relu(q, p, b):
+        need(V if q == "V" else S, q, "d%d_%d" % (p, b))
+        t = T["a%d" % p][:, b:1024:4]
+        if q == "V":
+            i = V.tensor_scalar(t, t, 0.0, 0.03125, AluOpType.max, AluOpType.mult)
+        else:
+            i = S.activation(t, t, ActivationFunctionType.Relu, scale=0.03125)
+        i.then_inc(T.sem["r%d_%d" % (p, b)], 1)
+
+    def quant_a(p):
+        need(V, "V", *["r%d_%d" % (p, b) for b in range(4)])
+        V.quantize_mx(T["aq%d" % p][:, 0:256], T["as%d" % p][:, 0:256], T["a%d" % p][:, 0:1024]).then_inc(T.sem["q%d" % p], 1)
+
+    def steps(q, text):
+        for w in text.replace("%", str(role - 1)).split():
+            k, d = w[0], [int(c) for c in w[1:] if c.isdigit()]
+            if w == "kf":
+                keypos()
+            elif w == "qvv":
+                quant("vv")
+            elif k == "q":
+                quant_a(d[0])
+            elif k == "p":
+                product("p", (0, 1, 2), "p%d" % d[0], "c%d" % d[0], d[0], "r%s", rt_ready)
+            elif k == "s":
+                product("s", (3, 4, 5, 6), "s%d_%d" % (d[0], d[1]), "d%d_%d" % (d[0], d[1]), d[1], "x%s" + str(d[0]), query_ready[d[0]])
+            elif k == "c":
+                copy_p(q, d[0])
+            elif k == "g":
+                pick(q, d[0], d[1])
+            elif k == "o":
+                offsets(d[0], d[1])
+            elif k == "d":
+                add(d[0], d[1])
+            elif k == "r":
+                relu(q, d[0], d[1])
+
+    if is_rank:
+        need(V, "V", "l_pos")
+        V.tensor_copy(T.pu[:], T.pz[:]).then_inc(T.sem.pu, 1)
+        for n in QUANTS:
+            quant(n)
+    kind = min(role, 1)
+    steps("E", TENSOR[kind])
+    steps("V", VECTOR[kind])
+    steps("S", SCALAR[kind])
+
+    if role == 1:
+        need(g, "g", "n_pt")
+        fused(positions(team(own)[2], every, "n_pt", "pt", "pt"))
+        need(g, "g", "n_r")
+        for n in "qs":
+            fused(put(n, team(own)[2], every, "n_r", "r%s", "r%s"))
+        for h in range(2):
+            need(g, "g", "n_k%d" % h)
+            for n in "qs":
+                fused(put(n, team(own)[2], every, "n_k%d" % h, "k%s1", "k%s1", 256 * h, 256 * h + 256))
+        tile_out(0, own, "t")
+    elif role == 2:
+        need(g, "g", "n_pp")
+        fused(positions(own, every, "n_pp", "pp", "pp"))
+        tile_out(1, partner, "h")
+    else:
+        need(g, "g", "pu")
+        fused(positions(team(twin)[1], off, "n_pt", "pt", "pu"), positions(team(own)[1], on[:half], "n_ph", "ph", "pu"),
+              positions(team(partner)[2], on[half:], "n_pp", "pp", "pu"))
+        for what in SENDS:
+            send(what)
+        tile_out(1, partner, "p")
+        source = {"own": (0, "a%s0", "q_vv", "q0"), "p": (1, "b%s_p", "n_v1", "n_ap"), "t": (2, "b%s_t", "n_v2", "n_at"), "h": (3, "b%s_h", "n_v3", "n_ah")}
+        for i, name in enumerate(YORDER):
+            v, a, ready, made = source[name]
+            need(E, "E", ready, made)
+            y = E.matmul_mx(T.ps7[:, 0:256], T["vq%d" % v][:, 0:128], T["vs%d" % v][:, 0:128], T[a % "q"][:, 0:256], T[a % "s"][:, 0:256], i == 0, i == 3)
+        y.then_inc(T.sem.ydone, 1)
+        need(S, "S", "ydone")
+        S.activation(T.yo[:], T.ps7[:, 0:256], ActivationFunctionType.Copy).then_inc(T.sem.ycopy, 1)
+        g.sync.wait_ge(T.sem.ycopy, 1)
+        g.sync.dma_start(T.y[:], T.yo[:]).then_inc(T.sem.ystore, 16)
+        g.sync.wait_ge(T.sem.ystore, 16)
+    g.wait_ge(T.sem.sent, sent[0])

@@ -7,50 +7,45 @@ SCRATCH = {
     "qx_b": ("sbuf", [128, 1024], "bfloat16"),
     "rt_b": ("sbuf", [128, 1024], "bfloat16"),
     "vv_b": ("sbuf", [128, 512], "bfloat16"),
-    "pz": ("sbuf", [128, 20], "int32"),
-    "pu": ("sbuf", [128, 20], "uint16"),
-    "pt": ("sbuf", [128, 20], "uint16"),
-    "ph": ("sbuf", [128, 20], "uint16"),
-    "pp": ("sbuf", [128, 20], "uint16"),
-    "kf": ("sbuf", [128, 4], "float32"),
-    "of0": ("sbuf", [128, 64], "uint16"),
-    "of1": ("sbuf", [128, 64], "uint16"),
-    "kq0": ("sbuf", [128, 512], CODES), "ks0": ("sbuf", [128, 512], "uint8"),
-    "kq1": ("sbuf", [128, 512], CODES), "ks1": ("sbuf", [128, 512], "uint8"),
-    "xq0": ("sbuf", [128, 256], CODES), "xs0": ("sbuf", [128, 256], "uint8"),
-    "xq1": ("sbuf", [128, 256], CODES), "xs1": ("sbuf", [128, 256], "uint8"),
-    "rq": ("sbuf", [128, 256], CODES), "rs": ("sbuf", [128, 256], "uint8"),
-    "pw": ("sbuf", [128, 1024], "float32"),
+    "kp0": ("sbuf", [128, 4], "int32"),
+    "kp1": ("sbuf", [128, 4], "int32"),
+    "qz": ("sbuf", [128, 16], "int32"),
+    "qu": ("sbuf", [128, 16], "uint16"),
+    "qn": ("sbuf", [128, 16], "uint16"),
+    "mq": ("sbuf", [128, 512], CODES), "ms": ("sbuf", [128, 512], "uint8"),
     "yo": ("sbuf", [128, 256], "float32"),
 }
 for _i in range(4):
     SCRATCH["vq%d" % _i] = ("sbuf", [128, 128], CODES)
     SCRATCH["vs%d" % _i] = ("sbuf", [128, 128], "uint8")
-for _p in range(2):
-    SCRATCH["u%d" % _p] = ("sbuf", [128, 1024], "float32")
-    SCRATCH["a%d" % _p] = ("sbuf", [128, 1024], "bfloat16")
-    SCRATCH["aq%d" % _p] = ("sbuf", [128, 256], CODES)
-    SCRATCH["as%d" % _p] = ("sbuf", [128, 256], "uint8")
-for _p in "pth":
+for _t in range(2):
+    SCRATCH["kq%d" % _t] = ("sbuf", [128, 512], CODES)
+    SCRATCH["ks%d" % _t] = ("sbuf", [128, 512], "uint8")
+    SCRATCH["kf%d" % _t] = ("sbuf", [128, 4], "float32")
+    SCRATCH["of%d" % _t] = ("sbuf", [128, 64], "uint16")
+    SCRATCH["pw%d" % _t] = ("sbuf", [128, 1024], "float32")
+    SCRATCH["u%d" % _t] = ("sbuf", [128, 1024], "float32")
+    SCRATCH["a%d" % _t] = ("sbuf", [128, 1024], "bfloat16")
+    SCRATCH["aq%d" % _t] = ("sbuf", [128, 256], CODES)
+    SCRATCH["as%d" % _t] = ("sbuf", [128, 256], "uint8")
+for _p in "pt":
     SCRATCH["bq_" + _p] = ("sbuf", [128, 256], CODES)
     SCRATCH["bs_" + _p] = ("sbuf", [128, 256], "uint8")
 for _i in range(8):
     SCRATCH["ps%d" % _i] = ("psum", [128, 512], "float32")
 
-SEMAPHORES = (["l_ky0", "l_ky1", "l_qx", "l_rt", "l_vv", "l_pos", "q_ky0", "q_ky1", "q_qx", "q_rt", "q_vv", "pu", "kf",
-               "n_pt", "n_ph", "n_pp", "n_k0", "n_k1", "n_r", "n_x", "n_v1", "n_v2", "n_v3", "n_ap", "n_at", "n_ah", "sent",
-               "ydone", "ycopy", "ystore", "q0", "q1"]
-              + ["p%d" % b for b in range(4)] + ["c%d" % b for b in range(4)]
-              + ["%s%d_%d" % (k, p, b) for k in "osgdr" for p in range(2) for b in range(4)])
+INPUTS = ["r", "x", "k0", "k1", "v"]
+SENDS = ["qp", "m", "k0", "k1", "v"]
+SEMAPHORES = (["l_" + n for n in INPUTS] + ["q_" + n for n in INPUTS]
+              + ["l_kp", "l_qp", "qu", "kf0", "kf1", "n_kp", "n_qp", "n_k0", "n_k1", "n_m", "n_v0", "n_v1", "n_v2", "n_v3",
+                 "n_ap", "n_at", "sent", "y0", "y1", "ycopy", "ystore", "q0", "q1"]
+              + ["%s%d%d" % (k, t, b) for k in "pcosgdr" for t in range(2) for b in range(4)])
 
-LOADS = ["ky0", "rt", "ky1", "qx", "vv"]
-QUANTS = ["ky0", "rt", "ky1", "qx"]
-SENDS = ["k0", "r", "k1", "x", "v"]
-TENSOR = ["p0 p1 s00 s01 p2 p3 s02 s03 s10 s11 s12 s13", "p0 p1 s%0 s%1 p2 p3 s%2 s%3"]
-SCALAR = ["c0 g00 g01 c2 g02 g03 g10 g11 g12 g13 r10 r11 r12", "c0 g%0 c2 g%2 r%0 r%1 r%2"]
-VECTOR = ["kf o00 o01 o02 o03 c1 d00 r00 d01 r01 c3 qvv o10 o11 o12 o13 d02 r02 d03 r03 q0 d10 d11 d12 d13 r13 q1",
-          "kf o%0 o%1 o%2 o%3 c1 g%1 d%0 d%1 c3 g%3 d%2 d%3 r%3 q%"]
-YORDER = ["own", "p", "t", "h"]
+OFFSETS = "kf% o%0 o%1 o%2 o%3 "
+TENSOR = "p%0 p%1 s%0 s%1 p%2 p%3 s%2 s%3 "
+ARRIVING = {"E": TENSOR, "S": "c%0 g%0 c%2 g%2 r%0 r%1 r%2 ", "V": OFFSETS + "c%1 g%1 d%0 d%1 c%3 g%3 d%2 d%3 r%3 q% "}
+OWN = {"E": TENSOR, "S": "c%0 g%0 g%1 g%2 g%3 r%1 r%2 ", "V": "Qr Qx Qk0 Qk1 " + OFFSETS + "c%1 d%0 c%2 c%3 Qv d%1 r%0 d%2 d%3 r%3 q% "}
+YORDER = ["own", "p", "t", "d"]
 
 
 def rank_program(g, core, T, topo):
@@ -60,29 +55,26 @@ def rank_program(g, core, T, topo):
         return
 
     def team(r):
-        return [r] + [c for c in topo.cores_of(r) if topo.die(c) == topo.die(r) and c != r][:2]
+        return [r] + [c for c in topo.cores_of(r) if topo.die(c) == topo.die(r) and c != r]
 
     own = [c for c in ranks if topo.die(c) == topo.die(core)][0]
-    if core not in team(own):
-        return
     role = team(own).index(core)
     is_rank = role == 0
     partner = [c for c in ranks if c != own][0]
     far = [c for c in T.cores if c not in here]
     twin = [c for c in far if topo.die(c) == topo.die(own)][0]
     diag = [c for c in far if c != twin][0]
+    _, H1, H2, H3 = team(own)
     off = topo.engines(own, twin)
     every = topo.engines(own, partner)
     on = [e for e in every if e not in off]
     half = len(off) // 2
 
-    direct = role == 1
-    count = {"l_pos": 9 * 16, "ystore": 16, "n_pt": len(off if direct else every), "n_ph": half, "n_pp": len(every) if is_rank else half,
-             "n_k0": 2 * len(off if direct else every), "n_k1": 2 * len(off if direct else every), "n_r": 2 * len(on if direct else every),
-             "n_x": 2 * (len(off) if is_rank else half), "n_v1": 2 * len(on), "n_v2": 2 * half, "n_v3": 2 * half}
-    for n in ("n_ap", "n_at", "n_ah"):
-        count[n] = 2 * len(every)
-    for n in LOADS:
+    A, B = len(every), len(off)
+    count = {"l_qp": 32, "qu": 4, "ycopy": 2, "ystore": 16, "l_kp": 16, "n_kp": A if is_rank else B, "n_qp": A,
+             "n_k0": 2 * (A if is_rank else B), "n_k1": 2 * (A if is_rank else B), "n_m": 2 * A,
+             "n_v0": 2 * A, "n_v1": 2 * B, "n_v2": 2 * half, "n_v3": 2 * half, "n_ap": 2 * A, "n_at": 2 * A}
+    for n in INPUTS:
         count["l_" + n] = 16
     seen = set()
 
@@ -106,176 +98,157 @@ def rank_program(g, core, T, topo):
     def view(n, name, lo, hi):
         return T[name % n][:, lo:hi].bitcast(dt.uint8) if n == "q" else T[name % n][:, lo:hi]
 
-    def put(n, dst, engines, sem, out, src, lo=0, hi=256):
-        return xfer(dst, engines, sem, view(n, out, lo, hi), view(n, src, lo, hi))
-
-    def positions(dst, engines, sem, out, src):
-        return xfer(dst, engines, sem, T[out][:, 0:20], T[src][:, 0:20])
-
-    def tile_out(p, dst, key):
-        need(g, "g", "q%d" % p)
+    def ship(event, src, lo, hi, *places):
+        need(g, "g", event)
         for n in "qs":
-            fused(put(n, dst, every, "n_a" + key, "b%s_" + key, "a%s" + str(p)))
+            fused(*[xfer(dst, engines, sem, view(n, out, lo, hi), view(n, src, lo, hi)) for dst, engines, sem, out in places])
+
+    def positions(event, src, *places):
+        need(g, "g", event)
+        fused(*[xfer(dst, engines, sem, T[out][:], T[src][:]) for dst, engines, sem, out in places])
 
     def send(what):
         if what in ("k0", "k1"):
-            need(g, "g", "q_ky" + what[1])
             lo = 256 * int(what[1])
-            for n in "qs":
-                fused(put(n, team(twin)[1], off, "n_" + what, "k%s1", "k%s0", lo, lo + 256))
-        if what == "r":
-            need(g, "g", "q_rt")
-            for n in "qs":
-                fused(put(n, team(own)[1], on, "n_r", "r%s", "r%s"))
-        if what == "x":
-            need(g, "g", "q_qx")
-            for n in "qs":
-                fused(put(n, team(own)[1], on[:half], "n_x", "x%s0", "x%s0"), put(n, team(partner)[2], on[half:], "n_x", "x%s1", "x%s0"),
-                      put(n, partner, off, "n_x", "x%s1", "x%s0"))
+            ship("q_" + what, "k%s0", lo, lo + 256, (team(twin)[1], off, "n_" + what, "k%s1"), (team(partner)[2], on, "n_" + what, "k%s1"))
+        if what == "qp":
+            positions("qu", "qu", (H2, every, "n_qp", "qn"))
+        if what == "m":
+            need(g, "g", "q_r")
+            ship("q_x", "m%s", 0, 512, (H2, every, "n_m", "m%s"))
         if what == "v":
-            need(g, "g", "q_vv")
-            for n in "qs":
-                fused(put(n, twin, off[:half], "n_v2", "v%s2", "v%s0", 0, 128), put(n, diag, off[half:], "n_v3", "v%s3", "v%s0", 0, 128),
-                      put(n, partner, on, "n_v1", "v%s1", "v%s0", 0, 128))
+            ship("q_v", "v%s0", 0, 128, (H3, every, "n_v0", "v%s0"))
+
+    piece = {"r": ("rt", "m%s", 0, 0, 256), "k0": ("ky", "k%s0", 0, 0, 256), "k1": ("ky", "k%s0", 256, 256, 256),
+             "x": ("qx", "m%s", 0, 256, 256), "v": ("vv", "v%s0", 0, 0, 128)}
 
     if is_rank:
-        g.sync.dma_start(T.pz[:, 0:4], T.kp[:]).then_inc(T.sem["l_pos"], 16)
-        for i in range(8):
-            (S if i % 2 else g.sync).dma_start(T.pz[16 * i:16 * i + 16, 4:20], T.qp[:]).then_inc(T.sem["l_pos"], 16)
-        for n in LOADS:
-            out, src = {"ky0": (T.ky_b[:, 0:1024], T.ky[:, 0:1024]), "ky1": (T.ky_b[:, 1024:2048], T.ky[:, 1024:2048]), "rt": (T.rt_b[:], T.rt[:]),
-                        "qx": (T.qx_b[:], T.qx[:]), "vv": (T.vv_b[:], T.vv[:])}[n]
-            S.dma_start(out, src).then_inc(T.sem["l_" + n], 16)
+        S.dma_start(T.kp0[:], T.kp[:]).then_inc(T.sem.l_kp, 16)
+        for i in range(2):
+            g.sync.dma_start(T.qz[16 * i:16 * i + 16, :], T.qp[:]).then_inc(T.sem.l_qp, 16)
+        for n in INPUTS:
+            src, _, lo, _, w = piece[n]
+            S.dma_start(T[src + "_b"][:, 4 * lo:4 * lo + 4 * w], T[src][:, 4 * lo:4 * lo + 4 * w]).then_inc(T.sem["l_" + n], 16)
 
-    def quant(name):
-        need(V, "V", "l_" + name)
-        q, s, b, lo, n = {"ky0": ("kq0", "ks0", "ky_b", 0, 256), "ky1": ("kq0", "ks0", "ky_b", 256, 256), "qx": ("xq0", "xs0", "qx_b", 0, 256),
-                          "rt": ("rq", "rs", "rt_b", 0, 256), "vv": ("vq0", "vs0", "vv_b", 0, 128)}[name]
-        V.quantize_mx(T[q][:, lo:lo + n], T[s][:, lo:lo + n], T[b][:, 4 * lo:4 * lo + 4 * n]).then_inc(T.sem["q_" + name], 1)
+    def quant(n):
+        need(V, "V", "l_" + n)
+        src, out, lo, at, w = piece[n]
+        V.quantize_mx(T[out % "q"][:, at:at + w], T[out % "s"][:, at:at + w], T[src + "_b"][:, 4 * lo:4 * lo + 4 * w]).then_inc(T.sem["q_" + n], 1)
 
-    KQ, KS = (T.kq0, T.ks0) if is_rank else (T.kq1, T.ks1)
-    key_pos = (T.pu, "pu") if is_rank else (T.pt, "n_pt")
-    query_pos = ((T.pu, "pu") if is_rank else (T.ph, "n_ph"), (T.pp, "n_pp"))
-    query_ready = ("q_qx" if is_rank else "n_x", "n_x")
-    rt_ready = "q_rt" if is_rank else "n_r"
+    query_pos = (T.qu, "qu") if is_rank else (T.qn, "n_qp")
+    ready = {"s": "q_x", "p": "q_r"} if is_rank else {"s": "n_m", "p": "n_m"}
+    banks = {"p": (0, 1), "s": (2, 3, 4, 5)} if is_rank else {"p": (0, 1, 2, 3), "s": (4, 5, 6, 7)}
     held, turn, bank = {}, {"p": 0, "s": 0}, {}
 
-    def keypos():
-        need(V, "V", key_pos[1])
-        V.tensor_scalar(T.kf[:], key_pos[0][:, 0:4], 128.0, None, AluOpType.subtract).then_inc(T.sem.kf, 1)
+    def keypos(t):
+        need(V, "V", ("l_kp", "n_kp")[t])
+        V.tensor_scalar(T["kf%d" % t][:], T["kp%d" % t][:], 128.0, None, AluOpType.subtract).then_inc(T.sem["kf%d" % t], 1)
 
-    def offsets(p, b):
-        need(V, "V", query_pos[p][1], "kf")
-        V.tensor_scalar(T["of%d" % p][:, 16 * b:16 * b + 16], query_pos[p][0][:, 4:20], T.kf[:, b:b + 1], 255.0,
-                        AluOpType.subtract, AluOpType.min).then_inc(T.sem["o%d_%d" % (p, b)], 1)
+    def offsets(t, b):
+        need(V, "V", query_pos[1], "kf%d" % t)
+        V.tensor_scalar(T["of%d" % t][:, 16 * b:16 * b + 16], query_pos[0][:], T["kf%d" % t][:, b:b + 1], 255.0,
+                        AluOpType.subtract, AluOpType.min).then_inc(T.sem["o%d%d" % (t, b)], 1)
 
-    def product(kind, banks, name, free, b, moving, ready):
-        k = banks[turn[kind] % len(banks)]
+    def product(kind, t, b):
+        name, lo = "%s%d%d" % (kind, t, b), 256 * (kind == "s")
+        k = banks[kind][turn[kind] % len(banks[kind])]
         turn[kind] += 1
         if k in held:
             need(E, "E", held[k])
-        held[k] = free
+        held[k] = "%s%d%d" % ({"p": "c", "s": "d"}[kind], t, b)
         bank[name] = T["ps%d" % k]
-        need(E, "E", ready, ("q_ky%d" if is_rank else "n_k%d") % (b // 2))
-        E.matmul_mx(bank[name][:, 0:256], KQ[:, 128 * b:128 * b + 128], KS[:, 128 * b:128 * b + 128],
-                    T[moving % "q"][:, 0:256], T[moving % "s"][:, 0:256], True, True).then_inc(T.sem[name], 1)
+        need(E, "E", ("q_k%d", "n_k%d")[t] % (b // 2), ready[kind])
+        E.matmul_mx(bank[name][:, 0:256], T["kq%d" % t][:, 128 * b:128 * b + 128], T["ks%d" % t][:, 128 * b:128 * b + 128],
+                    T.mq[:, lo:lo + 256], T.ms[:, lo:lo + 256], True, True).then_inc(T.sem[name], 1)
 
-    def copy_p(q, b):
-        need(V if q == "V" else S, q, "p%d" % b)
-        out, src = T.pw[:, 256 * b:256 * b + 256], bank["p%d" % b][:, 0:256]
-        i = V.tensor_copy(out, src) if q == "V" else S.activation(out, src, ActivationFunctionType.Copy)
-        i.then_inc(T.sem["c%d" % b], 1)
+    def move(q, out, src):
+        return V.tensor_copy(out, src) if q == "V" else S.activation(out, src, ActivationFunctionType.Copy)
 
-    def pick(q, p, b):
-        out = T["u%d" % p][:, 256 * b:256 * b + 256]
-        src = T.pw[:, 256 * b:256 * b + 256].indirect(T["of%d" % p][:, 16 * b:16 * b + 16])
-        need(V if q == "V" else S, q, "c%d" % b, "o%d_%d" % (p, b))
-        i = V.tensor_copy(out, src) if q == "V" else S.activation(out, src, ActivationFunctionType.Copy)
-        i.then_inc(T.sem["g%d_%d" % (p, b)], 1)
+    def copy_p(q, t, b):
+        need(V if q == "V" else S, q, "p%d%d" % (t, b))
+        move(q, T["pw%d" % t][:, 256 * b:256 * b + 256], bank["p%d%d" % (t, b)][:, 0:256]).then_inc(T.sem["c%d%d" % (t, b)], 1)
 
-    def add(p, b):
-        need(V, "V", "s%d_%d" % (p, b), "g%d_%d" % (p, b))
-        V.tensor_tensor(T["a%d" % p][:, b:1024:4], bank["s%d_%d" % (p, b)][:, 0:256], T["u%d" % p][:, 256 * b:256 * b + 256],
-                        AluOpType.add).then_inc(T.sem["d%d_%d" % (p, b)], 1)
+    def pick(q, t, b):
+        need(V if q == "V" else S, q, "c%d%d" % (t, b), "o%d%d" % (t, b))
+        src = T["pw%d" % t][:, 256 * b:256 * b + 256].indirect(T["of%d" % t][:, 16 * b:16 * b + 16])
+        move(q, T["u%d" % t][:, 256 * b:256 * b + 256], src).then_inc(T.sem["g%d%d" % (t, b)], 1)
 
-    def relu(q, p, b):
-        need(V if q == "V" else S, q, "d%d_%d" % (p, b))
-        t = T["a%d" % p][:, b:1024:4]
+    def add(t, b):
+        need(V, "V", "s%d%d" % (t, b), "g%d%d" % (t, b))
+        V.tensor_tensor(T["a%d" % t][:, b:1024:4], bank["s%d%d" % (t, b)][:, 0:256], T["u%d" % t][:, 256 * b:256 * b + 256],
+                        AluOpType.add).then_inc(T.sem["d%d%d" % (t, b)], 1)
+
+    def relu(q, t, b):
+        need(V if q == "V" else S, q, "d%d%d" % (t, b))
+        a = T["a%d" % t][:, b:1024:4]
         if q == "V":
-            i = V.tensor_scalar(t, t, 0.0, 0.03125, AluOpType.max, AluOpType.mult)
+            i = V.tensor_scalar(a, a, 0.0, 0.03125, AluOpType.max, AluOpType.mult)
         else:
-            i = S.activation(t, t, ActivationFunctionType.Relu, scale=0.03125)
-        i.then_inc(T.sem["r%d_%d" % (p, b)], 1)
+            i = S.activation(a, a, ActivationFunctionType.Relu, scale=0.03125)
+        i.then_inc(T.sem["r%d%d" % (t, b)], 1)
 
-    def quant_a(p):
-        need(V, "V", *["r%d_%d" % (p, b) for b in range(4)])
-        V.quantize_mx(T["aq%d" % p][:, 0:256], T["as%d" % p][:, 0:256], T["a%d" % p][:, 0:1024]).then_inc(T.sem["q%d" % p], 1)
+    def quant_a(t):
+        need(V, "V", *["r%d%d" % (t, b) for b in range(4)])
+        V.quantize_mx(T["aq%d" % t][:], T["as%d" % t][:], T["a%d" % t][:]).then_inc(T.sem["q%d" % t], 1)
 
-    def steps(q, text):
-        for w in text.replace("%", str(role - 1)).split():
-            k, d = w[0], [int(c) for c in w[1:] if c.isdigit()]
-            if w == "kf":
-                keypos()
-            elif w == "qvv":
-                quant("vv")
-            elif k == "q":
-                quant_a(d[0])
-            elif k == "p":
-                product("p", (0, 1, 2), "p%d" % d[0], "c%d" % d[0], d[0], "r%s", rt_ready)
-            elif k == "s":
-                product("s", (3, 4, 5, 6), "s%d_%d" % (d[0], d[1]), "d%d_%d" % (d[0], d[1]), d[1], "x%s" + str(d[0]), query_ready[d[0]])
-            elif k == "c":
-                copy_p(q, d[0])
-            elif k == "g":
-                pick(q, d[0], d[1])
-            elif k == "o":
-                offsets(d[0], d[1])
-            elif k == "d":
-                add(d[0], d[1])
-            elif k == "r":
-                relu(q, d[0], d[1])
-
-    if is_rank:
-        need(V, "V", "l_pos")
-        V.tensor_copy(T.pu[:], T.pz[:]).then_inc(T.sem.pu, 1)
-        for n in QUANTS:
-            quant(n)
-    kind = min(role, 1)
-    steps("E", TENSOR[kind])
-    steps("V", VECTOR[kind])
-    steps("S", SCALAR[kind])
+    def tile(order, t):
+        for q in "EVS":
+            for w in order[q].replace("%", str(t)).split():
+                k, b = w[0], int(w[-1]) if w[-1].isdigit() else 0
+                if k == "Q":
+                    quant(w[1:])
+                elif k == "k":
+                    keypos(t)
+                elif k == "q":
+                    quant_a(t)
+                elif k in "ps":
+                    product(k, t, b)
+                elif k == "c":
+                    copy_p(q, t, b)
+                elif k == "g":
+                    pick(q, t, b)
+                elif k == "o":
+                    offsets(t, b)
+                elif k == "d":
+                    add(t, b)
+                elif k == "r":
+                    relu(q, t, b)
 
     if role == 1:
-        need(g, "g", "n_pt")
-        fused(positions(team(own)[2], every, "n_pt", "pt", "pt"))
-        need(g, "g", "n_r")
-        for n in "qs":
-            fused(put(n, team(own)[2], every, "n_r", "r%s", "r%s"))
+        tile(ARRIVING, 1)
+        positions("n_kp", "kp1", (partner, every, "n_kp", "kp1"))
         for h in range(2):
-            need(g, "g", "n_k%d" % h)
-            for n in "qs":
-                fused(put(n, team(own)[2], every, "n_k%d" % h, "k%s1", "k%s1", 256 * h, 256 * h + 256))
-        tile_out(0, own, "t")
+            ship("n_k%d" % h, "k%s1", 256 * h, 256 * h + 256, (partner, every, "n_k%d" % h, "k%s1"))
+        ship("q1", "a%s1", 0, 256, (own, every, "n_at", "b%s_t"))
     elif role == 2:
-        need(g, "g", "n_pp")
-        fused(positions(own, every, "n_pp", "pp", "pp"))
-        tile_out(1, partner, "h")
+        tile(ARRIVING, 1)
+        positions("n_qp", "qn", (H1, every, "n_qp", "qn"))
+        ship("n_m", "m%s", 0, 512, (H1, every, "n_m", "m%s"))
+        ship("q1", "a%s1", 0, 256, (own, every, "n_ap", "b%s_p"))
+    elif role == 3:
+        ship("n_v0", "v%s0", 0, 128, (twin, off[:half], "n_v2", "v%s2"), (diag, off[half:], "n_v3", "v%s3"), (partner, on, "n_v1", "v%s1"))
     else:
-        need(g, "g", "pu")
-        fused(positions(team(twin)[1], off, "n_pt", "pt", "pu"), positions(team(own)[1], on[:half], "n_ph", "ph", "pu"),
-              positions(team(partner)[2], on[half:], "n_pp", "pp", "pu"))
+        need(V, "V", "l_qp")
+        for i in range(4):
+            V.tensor_copy(T.qu[32 * i:32 * i + 32, :], T.qz[0:32, :]).then_inc(T.sem.qu, 1)
+        tile(OWN, 0)
+        tile(ARRIVING, 1)
+        positions("l_kp", "kp0", (team(twin)[1], off, "n_kp", "kp1"), (team(partner)[2], on, "n_kp", "kp1"))
         for what in SENDS:
             send(what)
-        tile_out(1, partner, "p")
-        source = {"own": (0, "a%s0", "q_vv", "q0"), "p": (1, "b%s_p", "n_v1", "n_ap"), "t": (2, "b%s_t", "n_v2", "n_at"), "h": (3, "b%s_h", "n_v3", "n_ah")}
+        source = {"own": (0, "a%s0", "q_v", "q0"), "p": (1, "b%s_p", "n_v1", "n_ap"), "t": (2, "b%s_t", "n_v2", "n_at"), "d": (3, "a%s1", "n_v3", "q1")}
         for i, name in enumerate(YORDER):
-            v, a, ready, made = source[name]
-            need(E, "E", ready, made)
-            y = E.matmul_mx(T.ps7[:, 0:256], T["vq%d" % v][:, 0:128], T["vs%d" % v][:, 0:128], T[a % "q"][:, 0:256], T[a % "s"][:, 0:256], i == 0, i == 3)
-        y.then_inc(T.sem.ydone, 1)
-        need(S, "S", "ydone")
-        S.activation(T.yo[:], T.ps7[:, 0:256], ActivationFunctionType.Copy).then_inc(T.sem.ycopy, 1)
-        g.sync.wait_ge(T.sem.ycopy, 1)
+            v, a, there, made = source[name]
+            need(E, "E", there, made)
+            for h in range(2):
+                y = E.matmul_mx(T["ps%d" % (6 + h)][:, 0:128], T["vq%d" % v][:], T["vs%d" % v][:], T[a % "q"][:, 128 * h:128 * h + 128],
+                                T[a % "s"][:, 128 * h:128 * h + 128], i == 0, i == 3)
+                if i == 3:
+                    y.then_inc(T.sem["y%d" % h], 1)
+        for h, q in enumerate("SV"):
+            need(V if q == "V" else S, q, "y%d" % h)
+            move(q, T.yo[:, 128 * h:128 * h + 128], T["ps%d" % (6 + h)][:, 0:128]).then_inc(T.sem.ycopy, 1)
+        g.sync.wait_ge(T.sem.ycopy, 2)
         g.sync.dma_start(T.y[:], T.yo[:]).then_inc(T.sem.ystore, 16)
         g.sync.wait_ge(T.sem.ystore, 16)
     g.wait_ge(T.sem.sent, sent[0])

from concourse.bass import DstId, RemoteDMATransfer
from concourse.mybir import dt, AluOpType, ActivationFunctionType

CODES = "float8_e4m3fn_x4"
SCRATCH = {
    "ky_b": ("sbuf", [128, 2048], "bfloat16"),
    "qx_b": ("sbuf", [128, 1024], "bfloat16"),
    "rt_b": ("sbuf", [128, 1024], "bfloat16"),
    "vv_b": ("sbuf", [128, 512], "bfloat16"),
    "kp0": ("sbuf", [128, 4], "int32"),
    "kp1": ("sbuf", [128, 4], "int32"),
    "qz": ("sbuf", [128, 16], "int32"),
    "qu": ("sbuf", [128, 16], "uint16"),
    "qn": ("sbuf", [128, 16], "uint16"),
    "mq": ("sbuf", [128, 512], CODES), "ms": ("sbuf", [128, 512], "uint8"),
    "yo": ("sbuf", [128, 256], "float32"),
}
for _i in range(4):
    SCRATCH["vq%d" % _i] = ("sbuf", [128, 128], CODES)
    SCRATCH["vs%d" % _i] = ("sbuf", [128, 128], "uint8")
for _t in range(2):
    SCRATCH["kq%d" % _t] = ("sbuf", [128, 512], CODES)
    SCRATCH["ks%d" % _t] = ("sbuf", [128, 512], "uint8")
    SCRATCH["kf%d" % _t] = ("sbuf", [128, 4], "float32")
    SCRATCH["of%d" % _t] = ("sbuf", [128, 64], "uint16")
    SCRATCH["pw%d" % _t] = ("sbuf", [128, 1024], "float32")
    SCRATCH["u%d" % _t] = ("sbuf", [128, 1024], "float32")
    SCRATCH["a%d" % _t] = ("sbuf", [128, 1024], "bfloat16")
    SCRATCH["aq%d" % _t] = ("sbuf", [128, 256], CODES)
    SCRATCH["as%d" % _t] = ("sbuf", [128, 256], "uint8")
for _p in "pt":
    SCRATCH["bq_" + _p] = ("sbuf", [128, 256], CODES)
    SCRATCH["bs_" + _p] = ("sbuf", [128, 256], "uint8")
for _i in range(8):
    SCRATCH["ps%d" % _i] = ("psum", [128, 512], "float32")

INPUTS = ["r", "x", "k0", "k1", "v"]
SENDS = ["qp", "m", "k0", "k1", "v"]
SEMAPHORES = (["l_" + n for n in INPUTS] + ["q_" + n for n in INPUTS]
              + ["l_kp", "l_qp", "qu", "kf0", "kf1", "n_kp", "n_qp", "n_k0", "n_k1", "n_m", "n_v0", "n_v1", "n_v2", "n_v3",
                 "n_ap", "n_at", "sent", "y0", "y1", "ycopy", "ystore", "q0", "q1"]
              + ["%s%d%d" % (k, t, b) for k in "pcosgdr" for t in range(2) for b in range(4)])

OFFSETS = "kf% o%0 o%1 o%2 o%3 "
TENSOR = "p%0 p%1 s%0 s%1 p%2 p%3 s%2 s%3 "
ARRIVING = {"E": TENSOR, "S": "c%0 g%0 c%2 g%2 r%0 r%1 r%2 ", "V": OFFSETS + "c%1 g%1 d%0 d%1 c%3 g%3 d%2 d%3 r%3 q% "}
OWN = {"E": TENSOR, "S": "c%0 g%0 g%1 g%2 g%3 r%1 r%2 ", "V": "Qr Qx Qk0 Qk1 " + OFFSETS + "c%1 d%0 c%2 c%3 Qv d%1 r%0 d%2 d%3 r%3 q% "}
YORDER = ["own", "p", "t", "d"]


def rank_program(g, core, T, topo):
    here = topo.cores_of(core)
    ranks = [c for c in T.cores if c in here]
    if not ranks:
        return

    def team(r):
        return [r] + [c for c in topo.cores_of(r) if topo.die(c) == topo.die(r) and c != r]

    own = [c for c in ranks if topo.die(c) == topo.die(core)][0]
    role = team(own).index(core)
    is_rank = role == 0
    partner = [c for c in ranks if c != own][0]
    far = [c for c in T.cores if c not in here]
    twin = [c for c in far if topo.die(c) == topo.die(own)][0]
    diag = [c for c in far if c != twin][0]
    _, H1, H2, H3 = team(own)
    off = topo.engines(own, twin)
    every = topo.engines(own, partner)
    on = [e for e in every if e not in off]
    half = len(off) // 2

    A, B = len(every), len(off)
    count = {"l_qp": 32, "qu": 4, "ycopy": 2, "ystore": 16, "l_kp": 16, "n_kp": A if is_rank else B, "n_qp": A,
             "n_k0": 2 * (A if is_rank else B), "n_k1": 2 * (A if is_rank else B), "n_m": 2 * A,
             "n_v0": 2 * A, "n_v1": 2 * B, "n_v2": 2 * half, "n_v3": 2 * half, "n_ap": 2 * A, "n_at": 2 * A}
    for n in INPUTS:
        count["l_" + n] = 16
    seen = set()

    def need(queue, tag, *events):
        for e in events:
            if (tag, e) not in seen:
                seen.add((tag, e))
                queue.wait_ge(T.sem[e], count.get(e, 1))

    V, S, E = g.vector, g.scalar, g.tensor
    sent = [0]

    def xfer(dst, engines, sem, out, src):
        rid, pid = topo.addr(dst, core)
        sent[0] += len(engines)
        return RemoteDMATransfer(dst_ids=[DstId(rid=rid, pnc=pid)], dma_engine_mask=sum(1 << e for e in engines), remote_sem=T.sem[sem], srcs=[src], dsts=[out])

    def fused(*transfers):
        g.remote_dma_fused(list(transfers), local_sem=T.sem.sent)

    def view(n, name, lo, hi):
        return T[name % n][:, lo:hi].bitcast(dt.uint8) if n == "q" else T[name % n][:, lo:hi]

    def ship(event, src, lo, hi, *places):
        need(g, "g", event)
        for n in "qs":
            fused(*[xfer(dst, engines, sem, view(n, out, lo, hi), view(n, src, lo, hi)) for dst, engines, sem, out in places])

    def positions(event, src, *places):
        need(g, "g", event)
        fused(*[xfer(dst, engines, sem, T[out][:], T[src][:]) for dst, engines, sem, out in places])

    def send(what):
        if what in ("k0", "k1"):
            lo = 256 * int(what[1])
            ship("q_" + what, "k%s0", lo, lo + 256, (team(twin)[1], off, "n_" + what, "k%s1"), (team(partner)[2], on, "n_" + what, "k%s1"))
        if what == "qp":
            positions("qu", "qu", (H2, every, "n_qp", "qn"))
        if what == "m":
            need(g, "g", "q_r")
            ship("q_x", "m%s", 0, 512, (H2, every, "n_m", "m%s"))
        if what == "v":
            ship("q_v", "v%s0", 0, 128, (H3, every, "n_v0", "v%s0"))

    piece = {"r": ("rt", "m%s", 0, 0, 256), "k0": ("ky", "k%s0", 0, 0, 256), "k1": ("ky", "k%s0", 256, 256, 256),
             "x": ("qx", "m%s", 0, 256, 256), "v": ("vv", "v%s0", 0, 0, 128)}

    if is_rank:
        S.dma_start(T.kp0[:], T.kp[:]).then_inc(T.sem.l_kp, 16)
        for i in range(2):
            g.sync.dma_start(T.qz[16 * i:16 * i + 16, :], T.qp[:]).then_inc(T.sem.l_qp, 16)
        for n in INPUTS:
            src, _, lo, _, w = piece[n]
            S.dma_start(T[src + "_b"][:, 4 * lo:4 * lo + 4 * w], T[src][:, 4 * lo:4 * lo + 4 * w]).then_inc(T.sem["l_" + n], 16)

    def quant(n):
        need(V, "V", "l_" + n)
        src, out, lo, at, w = piece[n]
        V.quantize_mx(T[out % "q"][:, at:at + w], T[out % "s"][:, at:at + w], T[src + "_b"][:, 4 * lo:4 * lo + 4 * w]).then_inc(T.sem["q_" + n], 1)

    query_pos = (T.qu, "qu") if is_rank else (T.qn, "n_qp")
    ready = {"s": "q_x", "p": "q_r"} if is_rank else {"s": "n_m", "p": "n_m"}
    banks = {"p": (0, 1), "s": (2, 3, 4, 5)} if is_rank else {"p": (0, 1, 2, 3), "s": (4, 5, 6, 7)}
    held, turn, bank = {}, {"p": 0, "s": 0}, {}

    def keypos(t):
        need(V, "V", ("l_kp", "n_kp")[t])
        V.tensor_scalar(T["kf%d" % t][:], T["kp%d" % t][:], 128.0, None, AluOpType.subtract).then_inc(T.sem["kf%d" % t], 1)

    def offsets(t, b):
        need(V, "V", query_pos[1], "kf%d" % t)
        V.tensor_scalar(T["of%d" % t][:, 16 * b:16 * b + 16], query_pos[0][:], T["kf%d" % t][:, b:b + 1], 255.0,
                        AluOpType.subtract, AluOpType.min).then_inc(T.sem["o%d%d" % (t, b)], 1)

    def product(kind, t, b):
        name, lo = "%s%d%d" % (kind, t, b), 256 * (kind == "s")
        k = banks[kind][turn[kind] % len(banks[kind])]
        turn[kind] += 1
        if k in held:
            need(E, "E", held[k])
        held[k] = "%s%d%d" % ({"p": "c", "s": "d"}[kind], t, b)
        bank[name] = T["ps%d" % k]
        need(E, "E", ("q_k%d", "n_k%d")[t] % (b // 2), ready[kind])
        E.matmul_mx(bank[name][:, 0:256], T["kq%d" % t][:, 128 * b:128 * b + 128], T["ks%d" % t][:, 128 * b:128 * b + 128],
                    T.mq[:, lo:lo + 256], T.ms[:, lo:lo + 256], True, True).then_inc(T.sem[name], 1)

    def move(q, out, src):
        return V.tensor_copy(out, src) if q == "V" else S.activation(out, src, ActivationFunctionType.Copy)

    def copy_p(q, t, b):
        need(V if q == "V" else S, q, "p%d%d" % (t, b))
        move(q, T["pw%d" % t][:, 256 * b:256 * b + 256], bank["p%d%d" % (t, b)][:, 0:256]).then_inc(T.sem["c%d%d" % (t, b)], 1)

    def pick(q, t, b):
        need(V if q == "V" else S, q, "c%d%d" % (t, b), "o%d%d" % (t, b))
        src = T["pw%d" % t][:, 256 * b:256 * b + 256].indirect(T["of%d" % t][:, 16 * b:16 * b + 16])
        move(q, T["u%d" % t][:, 256 * b:256 * b + 256], src).then_inc(T.sem["g%d%d" % (t, b)], 1)

    def add(t, b):
        need(V, "V", "s%d%d" % (t, b), "g%d%d" % (t, b))
        V.tensor_tensor(T["a%d" % t][:, b:1024:4], bank["s%d%d" % (t, b)][:, 0:256], T["u%d" % t][:, 256 * b:256 * b + 256],
                        AluOpType.add).then_inc(T.sem["d%d%d" % (t, b)], 1)

    def relu(q, t, b):
        need(V if q == "V" else S, q, "d%d%d" % (t, b))
        a = T["a%d" % t][:, b:1024:4]
        if q == "V":
            i = V.tensor_scalar(a, a, 0.0, 0.03125, AluOpType.max, AluOpType.mult)
        else:
            i = S.activation(a, a, ActivationFunctionType.Relu, scale=0.03125)
        i.then_inc(T.sem["r%d%d" % (t, b)], 1)

    def quant_a(t):
        need(V, "V", *["r%d%d" % (t, b) for b in range(4)])
        V.quantize_mx(T["aq%d" % t][:], T["as%d" % t][:], T["a%d" % t][:]).then_inc(T.sem["q%d" % t], 1)

    def tile(order, t):
        for q in "EVS":
            for w in order[q].replace("%", str(t)).split():
                k, b = w[0], int(w[-1]) if w[-1].isdigit() else 0
                if k == "Q":
                    quant(w[1:])
                elif k == "k":
                    keypos(t)
                elif k == "q":
                    quant_a(t)
                elif k in "ps":
                    product(k, t, b)
                elif k == "c":
                    copy_p(q, t, b)
                elif k == "g":
                    pick(q, t, b)
                elif k == "o":
                    offsets(t, b)
                elif k == "d":
                    add(t, b)
                elif k == "r":
                    relu(q, t, b)

    if role == 1:
        tile(ARRIVING, 1)
        positions("n_kp", "kp1", (partner, every, "n_kp", "kp1"))
        for h in range(2):
            ship("n_k%d" % h, "k%s1", 256 * h, 256 * h + 256, (partner, every, "n_k%d" % h, "k%s1"))
        ship("q1", "a%s1", 0, 256, (own, every, "n_at", "b%s_t"))
    elif role == 2:
        tile(ARRIVING, 1)
        positions("n_qp", "qn", (H1, every, "n_qp", "qn"))
        ship("n_m", "m%s", 0, 512, (H1, every, "n_m", "m%s"))
        ship("q1", "a%s1", 0, 256, (own, every, "n_ap", "b%s_p"))
    elif role == 3:
        ship("n_v0", "v%s0", 0, 128, (twin, off[:half], "n_v2", "v%s2"), (diag, off[half:], "n_v3", "v%s3"), (partner, on, "n_v1", "v%s1"))
    else:
        need(V, "V", "l_qp")
        for i in range(4):
            V.tensor_copy(T.qu[32 * i:32 * i + 32, :], T.qz[0:32, :]).then_inc(T.sem.qu, 1)
        tile(OWN, 0)
        tile(ARRIVING, 1)
        positions("l_kp", "kp0", (team(twin)[1], off, "n_kp", "kp1"), (team(partner)[2], on, "n_kp", "kp1"))
        for what in SENDS:
            send(what)
        source = {"own": (0, "a%s0", "q_v", "q0"), "p": (1, "b%s_p", "n_v1", "n_ap"), "t": (2, "b%s_t", "n_v2", "n_at"), "d": (3, "a%s1", "n_v3", "q1")}
        for i, name in enumerate(YORDER):
            v, a, there, made = source[name]
            need(E, "E", there, made)
            for h in range(2):
                y = E.matmul_mx(T["ps%d" % (6 + h)][:, 0:128], T["vq%d" % v][:], T["vs%d" % v][:], T[a % "q"][:, 128 * h:128 * h + 128],
                                T[a % "s"][:, 128 * h:128 * h + 128], i == 0, i == 3)
                if i == 3:
                    y.then_inc(T.sem["y%d" % h], 1)
        for h, q in enumerate("SV"):
            need(V if q == "V" else S, q, "y%d" % h)
            move(q, T.yo[:, 128 * h:128 * h + 128], T["ps%d" % (6 + h)][:, 0:128]).then_inc(T.sem.ycopy, 1)
        g.sync.wait_ge(T.sem.ycopy, 2)
        g.sync.dma_start(T.y[:], T.yo[:]).then_inc(T.sem.ystore, 16)
        g.sync.wait_ge(T.sem.ystore, 16)
    g.wait_ge(T.sem.sent, sent[0])
